import numpy as np
import ml_dtypes


def mxq(x, axis, fmt="e4m3"):
    dtype, down = {"e4m3": (ml_dtypes.float8_e4m3fn, 7), "e5m2": (ml_dtypes.float8_e5m2, 14)}[fmt]
    v = np.moveaxis(np.asarray(x, np.float32).astype(ml_dtypes.bfloat16).astype(np.float64), axis, -1)
    blocks = v.reshape(v.shape[:-1] + (-1, 32))
    amax = np.abs(blocks).max(-1, keepdims=True)
    byte = np.maximum(np.where(amax > 0, np.frexp(amax)[1] - 1 + 127, 0) - down, 1)
    scale = np.exp2(byte - 127.0)
    codes = (blocks / scale).astype(np.float32).astype(dtype).astype(np.float64)
    return np.moveaxis((codes * scale).reshape(v.shape), -1, axis)


WIDE = False


def mx_kscale(k):
    if not WIDE:
        return np.ones(k)
    levels = np.array([10, -10, 5, -5, 0])
    if k % 512:
        return np.exp2(np.random.permutation(np.resize(levels, k // 32))).repeat(32)
    a = np.empty((k // 512, 16))
    for p in range(k // 512):
        a[p, :8] = np.random.permutation(np.resize(levels, 8))
        for g in range(8):
            far = levels[np.abs(levels - a[p, g]) >= 10]
            a[p, g + 8] = far[np.random.randint(len(far))]
    return np.exp2(a.ravel()).repeat(32)


def f64(x):
    return np.asarray(x).astype(np.float64)


def striped(idx):
    return np.tile(idx.reshape(-1, 16).T, (8, 1)).astype(np.uint16)


def unstriped(offs):
    return offs[:16].T.reshape(-1).astype(np.int64)


E2M1 = np.array([0.0, 0.5, 1.0, 1.5, 2.0, 3.0, 4.0, 6.0, -0.0, -0.5, -1.0, -1.5, -2.0, -3.0, -4.0, -6.0])


def pack_weight(w, fmt):
    k, n = w.shape
    w = f64(np.asarray(w, np.float32).astype(ml_dtypes.bfloat16)).reshape(k // 32, 32, n)
    amax = np.abs(w).max(1)
    if fmt == "e4m3":
        byte = np.frexp(amax)[1] - 1 + 127 - 7
    else:
        mant, ex = np.frexp(amax / 6.0)
        byte = np.where(mant > 0.5, ex, ex - 1) + 127
    byte = np.clip(np.where(amax > 0, byte, 1), 1, 254)
    scaled = (w * np.exp2(127.0 - byte)[:, None, :]).reshape(k, n).astype(np.float32)
    by_word = np.ascontiguousarray(scaled.reshape(k // 512, 128, 4, n).transpose(0, 1, 3, 2))
    if fmt == "e4m3":
        words = by_word.astype(ml_dtypes.float8_e4m3fn).view(np.uint8)
    else:
        c = by_word.astype(ml_dtypes.float4_e2m1fn).view(np.uint8) & 0xF
        words = (c[..., 0::2] | (c[..., 1::2] << 4)).reshape(k // 512, 128, 2 * n)
    return np.ascontiguousarray(words), np.ascontiguousarray(byte.astype(np.uint8).reshape(k // 512, 16, n))


def unpack_weight(words, scales, fmt):
    g, _, n = scales.shape
    words = np.ascontiguousarray(words).reshape(g, 128, n, -1)
    if fmt == "e4m3":
        vals = words.view(ml_dtypes.float8_e4m3fn).astype(np.float64)
    else:
        nib = np.empty((g, 128, n, 4), np.uint8)
        nib[..., 0::2] = words & 0xF
        nib[..., 1::2] = words >> 4
        vals = E2M1[nib]
    vals = vals * np.repeat(np.exp2(scales.astype(np.float64) - 127.0), 8, axis=1)[..., None]
    return vals.transpose(0, 1, 3, 2).reshape(g * 512, n)


def gelu(v):
    return 0.5 * v * (1.0 + np.tanh(np.sqrt(2.0 / np.pi) * (v + 0.044715 * v**3)))


def bf(x):
    return np.asarray(x, np.float32).astype(ml_dtypes.bfloat16)


def planes(Y):
    n, m = Y.shape
    b = f64(bf(Y)).reshape(n // 32, 32, m)
    amax = np.abs(b).max(1)
    byte = np.clip(np.where(amax > 0, np.frexp(amax)[1] - 1 + 127 - 7, 1), 1, 254)
    codes = (b * np.exp2(127.0 - byte)[:, None, :]).reshape(n, m).astype(np.float32).astype(ml_dtypes.float8_e4m3fn).view(np.uint8)
    words = codes.reshape(n // 512, 128, 4, m).transpose(0, 1, 3, 2)
    return np.ascontiguousarray(words), np.ascontiguousarray(byte.astype(np.uint8).reshape(n // 512, 16, m))


K, T, S, P, H, N = 1024, 4096, 1024, 512, 1024, 512

def setup_inputs():
    n = np.random.standard_normal
    s = mx_kscale(K)[:, None]
    u = mx_kscale(H)[:, None]
    d = {}
    d["tab_words"], d["tab_scales"] = pack_weight(n((K, T)) * s, "e2m1")
    d["offs"] = striped(np.random.permutation(T)[:S])
    d["pos1"] = striped(np.random.permutation(S)[:P])
    d["pos2"] = striped(np.random.permutation(S)[:P])
    d["w1"] = (n((K, H)) / K ** 0.5 / s).astype(np.float32)
    d["rgain"] = (1.3 * np.exp(0.3 * n(H))).astype(np.float32)
    d["ugain"] = (np.exp(0.3 * n(H)) * u[:, 0]).astype(np.float32)
    w2 = n((H, N)) / H ** 0.5 / u * np.exp(0.8 * n(N))
    d["w2_words"], d["w2_scales"] = pack_weight(w2, "e2m1")
    return d

def reference(tab_words, tab_scales, offs, pos1, pos2, w1, rgain, ugain, w2_words, w2_scales):
    v = unpack_weight(tab_words, tab_scales, "e2m1")[:, unstriped(offs)]
    h = f64(rgain)[:, None] * (mxq(f64(w1), 0, "e4m3").T @ v)
    scion = h[:, unstriped(pos1)]
    stock = h[:, unstriped(pos2)]
    z = np.maximum(scion, stock) + np.tanh(np.minimum(scion, stock))
    zq = mxq(f64(ugain)[:, None] * z, 0, "e4m3")
    y = unpack_weight(w2_words, w2_scales, "e2m1").T @ zq
    words, scales = planes(y)
    return y, words, scales

@@ -1,0 +1,261 @@
+from contextlib import ExitStack
+
+import concourse.mybir as mybir
+
+K, T, S, PAIRS, H, N = 1024, 4096, 1024, 512, 1024, 512
+FLOPS = 2 * K * H * S + 2 * H * N * PAIRS
+
+F32 = mybir.dt.float32
+BF16 = mybir.dt.bfloat16
+I32 = mybir.dt.int32
+U32 = mybir.dt.uint32
+U16 = mybir.dt.uint16
+U8 = mybir.dt.uint8
+FP8X4 = mybir.dt.float8_e4m3fn_x4
+FP4X4 = mybir.dt.float4_e2m1fn_x4
+ALU = mybir.AluOpType
+ACT = mybir.ActivationFunctionType
+
+P = 128
+PACK = 4
+PASS = P * PACK
+BANK = 512
+CHUNK = 128
+STEP = 512
+LIST_ROWS = 16
+UNITS = ((0, 0, 512), (1, 0, 256), (1, 256, 256))
+
+
+def tile_list_graft_union_features_kernel(
+    tc, tab_words, tab_scales, offs, pos1, pos2, w1, rgain, ugain, w2_words, w2_scales, out_0, out_1, out_2
+):
+    nc = tc.nc
+    with ExitStack() as ctx:
+        keep = ctx.enter_context(tc.tile_pool(name="keep", bufs=1))
+        ring = ctx.enter_context(tc.tile_pool(name="ring", bufs=3))
+        shared = ctx.enter_context(tc.tile_pool(name="shared", bufs=1))
+        psum_h = ctx.enter_context(tc.psum_pool(name="psum_h", bufs=6))
+        psum_y = ctx.enter_context(tc.psum_pool(name="psum_y", bufs=2))
+
+        offs_sb = keep.tile([P, S // LIST_ROWS], U16, name="offs_sb")
+        pos1_sb = keep.tile([P, PAIRS // LIST_ROWS], U16, name="pos1_sb")
+        pos2_sb = keep.tile([P, PAIRS // LIST_ROWS], U16, name="pos2_sb")
+        tab_w = [shared.tile([P, T], U16, name="tab_w0", align_bytes=64, offset=0)]
+        tab_s = shared.tile([P, T], U8, name="tab_s", align_bytes=64, offset=2 * T)
+        moved_s = keep.tile([P, S], U8, name="v_s1", align_bytes=64)
+        w1_raw = {}
+        w1_c = {}
+        w1_s = {}
+        y_s = keep.tile([P, PAIRS], U8, name="y_s", align_bytes=64)
+
+        nc.vector.memset(tab_s[:, : T // 2].bitcast(I32), 0)
+        nc.gpsimd.memset(tab_s[:, T // 2 :].bitcast(I32), 0)
+        with tc.tile_pool(name="early", bufs=1) as early:
+            warm = early.tile([P, 1], F32, name="warm")
+            nc.gpsimd.memset(warm[:], 0.0)
+            nc.scalar.activation(warm[:], warm[:], ACT.Tanh)
+        late = ctx.enter_context(tc.tile_pool(name="late", bufs=1))
+        tab_w.append(late.tile([P, T], U16, name="tab_w1", align_bytes=64))
+        rg = late.tile([P, 2, PACK], F32, name="rg")
+        nc.gpsimd.memset(moved_s[:].bitcast(I32), 0)
+
+        def load_w1(pool, b, a):
+            w1_raw[b, a] = pool.tile([P, PACK, PASS], F32, name="w1_raw%d%d" % (b, a))
+            rows = w1[a * PASS : (a + 1) * PASS, b * PASS : (b + 1) * PASS]
+            nc.sync.dma_start(w1_raw[b, a][:], rows.rearrange("(p j) c -> p j c", j=PACK))
+
+        nc.sync.dma_start(offs_sb[:], offs)
+        nc.sync.dma_start(pos1_sb[:], pos1)
+        nc.sync.dma_start(pos2_sb[:], pos2)
+        nc.sync.dma_start(tab_w[0][:].bitcast(I32), tab_words[0].bitcast(I32))
+        load_w1(keep, 0, 0)
+        for r in range(4):
+            rows = tab_scales.bitcast(I32).rearrange("a (q r) n -> r q a n", r=4)[r]
+            nc.sync.dma_start(tab_s[r:P:16, :].bitcast(I32), rows)
+        nc.sync.dma_start(tab_w[1][:].bitcast(I32), tab_words[1].bitcast(I32))
+        load_w1(late, 0, 1)
+        nc.sync.dma_start(rg[:], rgain.rearrange("(b p t) -> p b t", b=2, t=PACK))
+
+        def round_w1(pool, b, a, u, on_vector):
+            grouped = pool.tile([P, 2, P, PACK], BF16, name="w1_grouped%d%d%d" % (b, a, u), align_bytes=64)
+            src = w1_raw[b, a][:].rearrange("p j (m t) -> p m j t", t=PACK)[:, :, :, 2 * u : 2 * u + 2]
+            dst = grouped[:].rearrange("p t m j -> p m j t")
+            if on_vector:
+                nc.vector.tensor_copy(dst, src)
+            else:
+                nc.scalar.copy(dst, src)
+            return grouped
+
+        def quantize_w1(b, a, u, grouped):
+            w1_c[b, a, u] = keep.tile([P, 2 * P], U32, name="w1_c%d%d%d" % (b, a, u), align_bytes=64)
+            if (b, a) == (0, 0):
+                w1_s[b, a, u] = shared.tile([P, 2 * P], U8, name="w1_s00%d" % u, align_bytes=64, offset=2 * T + 256 * u)
+            else:
+                w1_s[b, a, u] = keep.tile([P, 2 * P], U8, name="w1_s%d%d%d" % (b, a, u), align_bytes=64)
+            nc.vector.quantize_mx(
+                w1_c[b, a, u][:].bitcast(FP8X4), w1_s[b, a, u][:], grouped[:].rearrange("p t m j -> p (t m j)")
+            )
+
+        h = {}
+
+        def first_product(b, t):
+            h[b, t] = keep.tile([P, S], F32, name="h%d%d" % (b, t))
+            u, cols = t // 2, slice((t % 2) * P, (t % 2 + 1) * P)
+            for m0 in range(0, S, BANK):
+                acc = psum_h.tile([P, BANK], F32, name="acc_h")
+                for a in range(2):
+                    nc.tensor.matmul_mx(
+                        acc[:],
+                        lhsT=w1_c[b, a, u][:, cols].bitcast(FP8X4),
+                        lhsT_scale=w1_s[b, a, u][:, cols],
+                        rhs=v_w[a][:, m0 : m0 + BANK].bitcast(FP4X4),
+                        rhs_scale=v_s[a][:, m0 : m0 + BANK],
+                        start=(a == 0),
+                        stop=(a == 1),
+                    )
+                nc.scalar.activation(h[b, t][:, m0 : m0 + BANK], acc[:], ACT.Copy, scale=rg[:, b, t : t + 1])
+
+        def deal_w2(a):
+            nc.vector.tensor_copy(
+                w2w[a][:].bitcast(U16).rearrange("p (r q) -> p q r", r=PACK),
+                w2w_raw[:, a, :].bitcast(U16).rearrange("p (q r) -> p q r", r=PACK),
+            )
+            nc.vector.tensor_copy(
+                w2s[a][:].rearrange("p (r q) -> p q r", r=PACK),
+                w2s_raw[:, a, :].rearrange("p (q r) -> p q r", r=PACK),
+            )
+
+        v_w = [keep.tile([P, S], U16, name="v_w0", align_bytes=64)]
+        nc.vector.tensor_copy(v_w[0][:], tab_w[0][:].indirect(offs_sb[:]))
+        v_s = [shared.tile([P, S], U8, name="v_s0", align_bytes=64, offset=0), moved_s]
+        nc.vector.tensor_copy(v_s[0][:], tab_s[:].indirect(offs_sb[:]))
+        nc.sync.dma_start(v_s[1][0:100, :].bitcast(I32), v_s[0][16:116, :].bitcast(I32))
+        w2s_raw = shared.tile([P, 2, N], U8, name="w2s_raw", align_bytes=64, offset=2 * T + 512)
+        w2w_raw = shared.tile([P, 2, 2 * N], U8, name="w2w_raw", align_bytes=64, offset=2 * T + 1536)
+        nc.gpsimd.memset(w2s_raw[:].rearrange("p a n -> p (a n)").bitcast(I32), 0)
+        nc.sync.dma_start(w2w_raw[:].bitcast(I32), w2_words.bitcast(I32).rearrange("a p n -> p a n"))
+        for q in range(4):
+            nc.sync.dma_start(
+                w2s_raw[32 * q : 32 * q + 4, :, :].bitcast(I32),
+                w2_scales.bitcast(I32)[:, 4 * q : 4 * q + 4, :].rearrange("a r n -> r a n"),
+            )
+        with tc.tile_pool(name="head", bufs=1) as head:
+            first = [round_w1(head, 0, 0, u, False) for u in range(2)]
+            v_w.append(shared.tile([P, S], U16, name="v_w1", align_bytes=64, offset=2 * T + 3584))
+            nc.vector.tensor_copy(v_w[1][:], tab_w[1][:].indirect(offs_sb[:]))
+            for u in range(2):
+                quantize_w1(0, 0, u, first[u])
+            for u in range(2):
+                quantize_w1(0, 1, u, round_w1(head, 0, 1, u, u == 1))
+        body = ctx.enter_context(tc.tile_pool(name="body", bufs=1))
+        ug = body.tile([P, 2, PACK], F32, name="ug")
+        nc.sync.dma_start(ug[:], ugain.rearrange("(b p t) -> p b t", b=2, t=PACK))
+        for a in range(2):
+            load_w1(body, 1, a)
+        w2w = [body.tile([P, 2 * N], U8, name="w2w%d" % a, align_bytes=64) for a in range(2)]
+        w2s = [body.tile([P, N], U8, name="w2s%d" % a, align_bytes=64) for a in range(2)]
+        for t in range(PACK):
+            first_product(0, t)
+        for a in range(2):
+            deal_w2(a)
+
+        z_planes = {}
+        z_c = {}
+        z_s = {}
+
+        def pick(b, j0, width, t0):
+            scion = ring.tile([P, STEP], F32, name="scion")
+            stock = ring.tile([P, STEP], F32, name="stock")
+            entries = slice(j0 // LIST_ROWS, (j0 + width) // LIST_ROWS)
+            for i in range(STEP // width):
+                cols = slice(i * width, (i + 1) * width)
+                nc.vector.tensor_copy(scion[:, cols], h[b, t0 + i][:].indirect(pos1_sb[:, entries]))
+                nc.vector.tensor_copy(stock[:, cols], h[b, t0 + i][:].indirect(pos2_sb[:, entries]))
+            weak = ring.tile([P, STEP], F32, name="weak")
+            strong = ring.tile([P, STEP], F32, name="strong")
+            bounded = ring.tile([P, STEP], F32, name="bounded")
+            nc.vector.tensor_tensor(weak[:], scion[:], stock[:], ALU.min)
+            nc.vector.tensor_tensor(strong[:], scion[:], stock[:], ALU.max)
+            nc.scalar.activation(bounded[:], weak[:], ACT.Tanh)
+            return strong, bounded
+
+        def join(b, j0, width, t0, strong, bounded):
+            total = ring.tile([P, STEP], F32, name="total")
+            nc.vector.tensor_tensor(total[:], strong[:], bounded[:], ALU.add)
+            if t0 == 0:
+                z_planes[b, j0] = keep.tile([P, PACK, width], BF16, name="z_planes%d_%d" % (b, j0))
+            for i in range(STEP // width):
+                t = t0 + i
+                nc.scalar.activation(
+                    z_planes[b, j0][:, t, :], total[:, i * width : (i + 1) * width], ACT.Copy, scale=ug[:, b, t : t + 1]
+                )
+
+        def quantize_z(b, j0, width):
+            grouped = keep.tile([P, width, PACK], BF16, name="z_grouped%d_%d" % (b, j0), align_bytes=64)
+            nc.scalar.copy(
+                grouped[:].rearrange("p (c i) t -> p c t i", i=4),
+                z_planes[b, j0][:].rearrange("p t (c i) -> p c t i", i=4),
+            )
+            codes = keep.tile([P, width], U32, name="z_c%d_%d" % (b, j0), align_bytes=64)
+            scales = keep.tile([P, width], U8, name="z_s%d_%d" % (b, j0), align_bytes=64)
+            nc.vector.quantize_mx(codes[:].bitcast(FP8X4), scales[:], grouped[:].rearrange("p c t -> p (c t)"))
+            for c0 in range(0, width, CHUNK):
+                z_c[b, j0 + c0] = codes[:, c0 : c0 + CHUNK]
+                z_s[b, j0 + c0] = scales[:, c0 : c0 + CHUNK]
+
+        def second_product(j0, width, last):
+            y = keep.tile([P, PACK, width], F32, name="y%d" % j0)
+            grouped = keep.tile([P, width, PACK], BF16, name="y_grouped%d" % j0, align_bytes=64)
+            codes = keep.tile([P, width], U32, name="y_c%d" % j0, align_bytes=64)
+            for c0 in range(0, width, CHUNK):
+                acc = psum_y.tile([P, PACK, CHUNK], F32, name="acc_y")
+                for t in range(PACK):
+                    for b in range(2):
+                        nc.tensor.matmul_mx(
+                            acc[:, t, :],
+                            lhsT=w2w[b][:, 2 * P * t : 2 * P * (t + 1)].bitcast(FP4X4),
+                            lhsT_scale=w2s[b][:, P * t : P * (t + 1)],
+                            rhs=z_c[b, j0 + c0].bitcast(FP8X4),
+                            rhs_scale=z_s[b, j0 + c0],
+                            start=(b == 0),
+                            stop=(b == 1),
+                        )
+                nc.scalar.copy(y[:, :, c0 : c0 + CHUNK], acc[:])
+            dst = grouped[:].rearrange("p (c i) t -> p c t i", i=4)
+            src = y[:].rearrange("p t (c i) -> p c t i", i=4)
+            if last:
+                nc.vector.tensor_copy(dst, src)
+            else:
+                nc.scalar.copy(dst, src)
+            nc.sync.dma_start(out_0.rearrange("(p t) j -> p t j", t=PACK)[:, :, j0 : j0 + width], y[:])
+            nc.vector.quantize_mx(
+                codes[:].bitcast(FP8X4), y_s[:, j0 : j0 + width], grouped[:].rearrange("p c t -> p (c t)")
+            )
+            words = out_1[0].rearrange("p m t -> p (m t)")[:, PACK * j0 : PACK * (j0 + width)]
+            nc.sync.dma_start(words.bitcast(I32), codes[:].bitcast(I32))
+
+        steps = [(b, j0, width, t0) for b, j0, width in UNITS for t0 in range(0, PACK, STEP // width)]
+        later_w1 = {}
+        pending = None
+        for i, step in enumerate(steps + [None]):
+            picked = pick(*step) if step is not None else None
+            if i < 2:
+                later_w1[i] = [round_w1(body, 1, i, u, False) for u in range(2)]
+            if 1 <= i < 3:
+                for u in range(2):
+                    quantize_w1(1, i - 1, u, later_w1[i - 1][u])
+            if i == 2:
+                for t in range(PACK):
+                    first_product(1, t)
+            if pending is not None:
+                (b, j0, width, t0), values = pending
+                join(b, j0, width, t0, *values)
+                if t0 + STEP // width == PACK:
+                    quantize_z(b, j0, width)
+                    if b == 1:
+                        second_product(j0, width, step is None)
+            pending = (step, picked)
+
+        for q in range(4):
+            engine = nc.scalar if q % 2 else nc.sync
+            engine.dma_start(out_2[0, 4 * q : 4 * q + 4, :].bitcast(I32), y_s[32 * q : 32 * q + 4, :].bitcast(I32))

@@ -21,9 +21,8 @@ PACK = 4
 PASS = P * PACK
 BANK = 512
 CHUNK = 128
-STEP = 512
 LIST_ROWS = 16
-UNITS = ((0, 0, 512), (1, 0, 256), (1, 256, 256))
+UNITS = ((0, 0, 512, 2), (1, 0, 256, 4), (1, 256, 128, 4), (1, 384, 128, 2))
 
 
 def tile_list_graft_union_features_kernel(
@@ -32,7 +31,7 @@ def tile_list_graft_union_features_kernel(
     nc = tc.nc
     with ExitStack() as ctx:
         keep = ctx.enter_context(tc.tile_pool(name="keep", bufs=1))
-        ring = ctx.enter_context(tc.tile_pool(name="ring", bufs=3))
+        ring = ctx.enter_context(tc.tile_pool(name="ring", bufs=2))
         shared = ctx.enter_context(tc.tile_pool(name="shared", bufs=1))
         psum_h = ctx.enter_context(tc.psum_pool(name="psum_h", bufs=6))
         psum_y = ctx.enter_context(tc.psum_pool(name="psum_y", bufs=2))
@@ -55,12 +54,12 @@ def tile_list_graft_union_features_kernel(
             nc.gpsimd.memset(warm[:], 0.0)
             nc.scalar.activation(warm[:], warm[:], ACT.Tanh)
         late = ctx.enter_context(tc.tile_pool(name="late", bufs=1))
-        tab_w.append(late.tile([P, T], U16, name="tab_w1", align_bytes=64))
+        tab_w.append(late.tile([P, T], U16, name="tab_w1", tag="second", align_bytes=64))
         rg = late.tile([P, 2, PACK], F32, name="rg")
         nc.gpsimd.memset(moved_s[:].bitcast(I32), 0)
 
-        def load_w1(pool, b, a):
-            w1_raw[b, a] = pool.tile([P, PACK, PASS], F32, name="w1_raw%d%d" % (b, a))
+        def load_w1(b, a, tag):
+            w1_raw[b, a] = late.tile([P, PACK, PASS], F32, name="w1_raw%d%d" % (b, a), tag=tag, align_bytes=64)
             rows = w1[a * PASS : (a + 1) * PASS, b * PASS : (b + 1) * PASS]
             nc.sync.dma_start(w1_raw[b, a][:], rows.rearrange("(p j) c -> p j c", j=PACK))
 
@@ -68,12 +67,12 @@ def tile_list_graft_union_features_kernel(
         nc.sync.dma_start(pos1_sb[:], pos1)
         nc.sync.dma_start(pos2_sb[:], pos2)
         nc.sync.dma_start(tab_w[0][:].bitcast(I32), tab_words[0].bitcast(I32))
-        load_w1(keep, 0, 0)
         for r in range(4):
             rows = tab_scales.bitcast(I32).rearrange("a (q r) n -> r q a n", r=4)[r]
             nc.sync.dma_start(tab_s[r:P:16, :].bitcast(I32), rows)
+        load_w1(0, 0, "first")
         nc.sync.dma_start(tab_w[1][:].bitcast(I32), tab_words[1].bitcast(I32))
-        load_w1(late, 0, 1)
+        load_w1(0, 1, "third")
         nc.sync.dma_start(rg[:], rgain.rearrange("(b p t) -> p b t", b=2, t=PACK))
 
         def round_w1(pool, b, a, u, on_vector):
@@ -117,21 +116,16 @@ def tile_list_graft_union_features_kernel(
 
         def deal_w2(a):
             nc.vector.tensor_copy(
-                w2w[a][:].bitcast(U16).rearrange("p (r q) -> p q r", r=PACK),
-                w2w_raw[:, a, :].bitcast(U16).rearrange("p (q r) -> p q r", r=PACK),
+                w2w[a][:].bitcast(U16).rearrange("p (r q) -> p r q", r=PACK),
+                w2w_raw[:, a, :].bitcast(U16).rearrange("p (q r) -> p r q", r=PACK),
             )
             nc.vector.tensor_copy(
-                w2s[a][:].rearrange("p (r q) -> p q r", r=PACK),
-                w2s_raw[:, a, :].rearrange("p (q r) -> p q r", r=PACK),
+                w2s[a][:].rearrange("p (r q) -> p r q", r=PACK),
+                w2s_raw[:, a, :].rearrange("p (q r) -> p r q", r=PACK),
             )
 
-        v_w = [keep.tile([P, S], U16, name="v_w0", align_bytes=64)]
-        nc.vector.tensor_copy(v_w[0][:], tab_w[0][:].indirect(offs_sb[:]))
-        v_s = [shared.tile([P, S], U8, name="v_s0", align_bytes=64, offset=0), moved_s]
-        nc.vector.tensor_copy(v_s[0][:], tab_s[:].indirect(offs_sb[:]))
-        nc.sync.dma_start(v_s[1][0:100, :].bitcast(I32), v_s[0][16:116, :].bitcast(I32))
-        w2s_raw = shared.tile([P, 2, N], U8, name="w2s_raw", align_bytes=64, offset=2 * T + 512)
-        w2w_raw = shared.tile([P, 2, 2 * N], U8, name="w2w_raw", align_bytes=64, offset=2 * T + 1536)
+        w2s_raw = late.tile([P, 2, N], U8, name="w2s_raw", align_bytes=64)
+        w2w_raw = late.tile([P, 2, 2 * N], U8, name="w2w_raw", align_bytes=64)
         nc.gpsimd.memset(w2s_raw[:].rearrange("p a n -> p (a n)").bitcast(I32), 0)
         nc.sync.dma_start(w2w_raw[:].bitcast(I32), w2_words.bitcast(I32).rearrange("a p n -> p a n"))
         for q in range(4):
@@ -139,22 +133,27 @@ def tile_list_graft_union_features_kernel(
                 w2s_raw[32 * q : 32 * q + 4, :, :].bitcast(I32),
                 w2_scales.bitcast(I32)[:, 4 * q : 4 * q + 4, :].rearrange("a r n -> r a n"),
             )
+        v_w = [keep.tile([P, S], U16, name="v_w0", align_bytes=64)]
+        nc.vector.tensor_copy(v_w[0][:], tab_w[0][:].indirect(offs_sb[:]))
+        v_s = [shared.tile([P, S], U8, name="v_s0", align_bytes=64, offset=0), moved_s]
+        nc.vector.tensor_copy(v_s[0][:], tab_s[:].indirect(offs_sb[:]))
+        nc.sync.dma_start(v_s[1][0:100, :].bitcast(I32), v_s[0][16:116, :].bitcast(I32))
         with tc.tile_pool(name="head", bufs=1) as head:
             first = [round_w1(head, 0, 0, u, False) for u in range(2)]
-            v_w.append(shared.tile([P, S], U16, name="v_w1", align_bytes=64, offset=2 * T + 3584))
+            v_w.append(shared.tile([P, S], U16, name="v_w1", align_bytes=64, offset=2 * T + 512))
             nc.vector.tensor_copy(v_w[1][:], tab_w[1][:].indirect(offs_sb[:]))
             for u in range(2):
                 quantize_w1(0, 0, u, first[u])
-            for u in range(2):
-                quantize_w1(0, 1, u, round_w1(head, 0, 1, u, u == 1))
+            load_w1(1, 0, "first")
+            load_w1(1, 1, "second")
+            quantize_w1(0, 1, 0, round_w1(head, 0, 1, 0, False))
+        quantize_w1(0, 1, 1, round_w1(late, 0, 1, 1, False))
         body = ctx.enter_context(tc.tile_pool(name="body", bufs=1))
         ug = body.tile([P, 2, PACK], F32, name="ug")
         nc.sync.dma_start(ug[:], ugain.rearrange("(b p t) -> p b t", b=2, t=PACK))
-        for a in range(2):
-            load_w1(body, 1, a)
         w2w = [body.tile([P, 2 * N], U8, name="w2w%d" % a, align_bytes=64) for a in range(2)]
         w2s = [body.tile([P, N], U8, name="w2s%d" % a, align_bytes=64) for a in range(2)]
-        for t in range(PACK):
+        for t in range(2):
             first_product(0, t)
         for a in range(2):
             deal_w2(a)
@@ -163,39 +162,52 @@ def tile_list_graft_union_features_kernel(
         z_c = {}
         z_s = {}
 
-        def pick(b, j0, width, t0):
-            scion = ring.tile([P, STEP], F32, name="scion")
-            stock = ring.tile([P, STEP], F32, name="stock")
+        def pick(b, j0, width, count, t0):
+            scion = ring.tile([P, count * width], F32, name="scion")
+            stock = ring.tile([P, count * width], F32, name="stock")
             entries = slice(j0 // LIST_ROWS, (j0 + width) // LIST_ROWS)
-            for i in range(STEP // width):
+            for i in range(count):
                 cols = slice(i * width, (i + 1) * width)
                 nc.vector.tensor_copy(scion[:, cols], h[b, t0 + i][:].indirect(pos1_sb[:, entries]))
                 nc.vector.tensor_copy(stock[:, cols], h[b, t0 + i][:].indirect(pos2_sb[:, entries]))
-            weak = ring.tile([P, STEP], F32, name="weak")
-            strong = ring.tile([P, STEP], F32, name="strong")
-            bounded = ring.tile([P, STEP], F32, name="bounded")
+            weak = ring.tile([P, count * width], F32, name="weak")
+            strong = ring.tile([P, count * width], F32, name="strong")
+            bounded = ring.tile([P, count * width], F32, name="bounded")
             nc.vector.tensor_tensor(weak[:], scion[:], stock[:], ALU.min)
             nc.vector.tensor_tensor(strong[:], scion[:], stock[:], ALU.max)
             nc.scalar.activation(bounded[:], weak[:], ACT.Tanh)
             return strong, bounded
 
-        def join(b, j0, width, t0, strong, bounded):
-            total = ring.tile([P, STEP], F32, name="total")
+        def join(b, j0, width, count, t0, strong, bounded):
+            total = ring.tile([P, count * width], F32, name="total")
             nc.vector.tensor_tensor(total[:], strong[:], bounded[:], ALU.add)
             if t0 == 0:
                 z_planes[b, j0] = keep.tile([P, PACK, width], BF16, name="z_planes%d_%d" % (b, j0))
-            for i in range(STEP // width):
+            for i in range(count):
                 t = t0 + i
                 nc.scalar.activation(
                     z_planes[b, j0][:, t, :], total[:, i * width : (i + 1) * width], ACT.Copy, scale=ug[:, b, t : t + 1]
                 )
 
-        def quantize_z(b, j0, width):
+        def join_last(b, j0, width, count, t0, strong, bounded):
+            if t0 == 0:
+                z_planes[b, j0] = keep.tile([P, PACK * width], F32, name="z_sums")
+            nc.vector.tensor_tensor(z_planes[b, j0][:, t0 * width : (t0 + count) * width], strong[:], bounded[:], ALU.add)
+
+        def quantize_z(b, j0, width, last):
             grouped = keep.tile([P, width, PACK], BF16, name="z_grouped%d_%d" % (b, j0), align_bytes=64)
-            nc.scalar.copy(
-                grouped[:].rearrange("p (c i) t -> p c t i", i=4),
-                z_planes[b, j0][:].rearrange("p t (c i) -> p c t i", i=4),
-            )
+            if last:
+                nc.vector.tensor_tensor(
+                    grouped[:].rearrange("p (c i) t -> p c t i", i=2),
+                    z_planes[b, j0][:].rearrange("p (t c i) -> p c t i", t=PACK, i=2),
+                    ug[:, b, :].unsqueeze(1).unsqueeze(3).to_broadcast([P, width // 2, PACK, 2]),
+                    ALU.mult,
+                )
+            else:
+                nc.scalar.copy(
+                    grouped[:].rearrange("p (c i) t -> p c t i", i=4),
+                    z_planes[b, j0][:].rearrange("p t (c i) -> p c t i", i=4),
+                )
             codes = keep.tile([P, width], U32, name="z_c%d_%d" % (b, j0), align_bytes=64)
             scales = keep.tile([P, width], U8, name="z_s%d_%d" % (b, j0), align_bytes=64)
             nc.vector.quantize_mx(codes[:].bitcast(FP8X4), scales[:], grouped[:].rearrange("p c t -> p (c t)"))
@@ -208,11 +220,15 @@ def tile_list_graft_union_features_kernel(
             grouped = keep.tile([P, width, PACK], BF16, name="y_grouped%d" % j0, align_bytes=64)
             codes = keep.tile([P, width], U32, name="y_c%d" % j0, align_bytes=64)
             for c0 in range(0, width, CHUNK):
-                acc = psum_y.tile([P, PACK, CHUNK], F32, name="acc_y")
+                if last:
+                    sums = [psum_h.tile([P, BANK], F32, name="acc_h")[:, :CHUNK] for t in range(PACK)]
+                else:
+                    acc = psum_y.tile([P, PACK, CHUNK], F32, name="acc_y")
+                    sums = [acc[:, t, :] for t in range(PACK)]
                 for t in range(PACK):
                     for b in range(2):
                         nc.tensor.matmul_mx(
-                            acc[:, t, :],
+                            sums[t],
                             lhsT=w2w[b][:, 2 * P * t : 2 * P * (t + 1)].bitcast(FP4X4),
                             lhsT_scale=w2s[b][:, P * t : P * (t + 1)],
                             rhs=z_c[b, j0 + c0].bitcast(FP8X4),
@@ -220,7 +236,10 @@ def tile_list_graft_union_features_kernel(
                             start=(b == 0),
                             stop=(b == 1),
                         )
-                nc.scalar.copy(y[:, :, c0 : c0 + CHUNK], acc[:])
+                    if last:
+                        nc.scalar.copy(y[:, t, :], sums[t])
+                if not last:
+                    nc.scalar.copy(y[:, :, c0 : c0 + CHUNK], acc[:])
             dst = grouped[:].rearrange("p (c i) t -> p c t i", i=4)
             src = y[:].rearrange("p t (c i) -> p c t i", i=4)
             if last:
@@ -232,28 +251,31 @@ def tile_list_graft_union_features_kernel(
                 codes[:].bitcast(FP8X4), y_s[:, j0 : j0 + width], grouped[:].rearrange("p c t -> p (c t)")
             )
             words = out_1[0].rearrange("p m t -> p (m t)")[:, PACK * j0 : PACK * (j0 + width)]
-            nc.sync.dma_start(words.bitcast(I32), codes[:].bitcast(I32))
+            (nc.scalar if last else nc.sync).dma_start(words.bitcast(I32), codes[:].bitcast(I32))
 
-        steps = [(b, j0, width, t0) for b, j0, width in UNITS for t0 in range(0, PACK, STEP // width)]
-        later_w1 = {}
+        steps = [unit + (t0,) for unit in UNITS for t0 in range(0, PACK, unit[3])]
         pending = None
         for i, step in enumerate(steps + [None]):
+            if i < 2:
+                later_w1 = [round_w1(body, 1, a, i, False) for a in range(2)]
             picked = pick(*step) if step is not None else None
             if i < 2:
-                later_w1[i] = [round_w1(body, 1, i, u, False) for u in range(2)]
-            if 1 <= i < 3:
-                for u in range(2):
-                    quantize_w1(1, i - 1, u, later_w1[i - 1][u])
-            if i == 2:
+                for a in range(2):
+                    quantize_w1(1, a, i, later_w1[a])
+            if i == 0:
+                for t in range(2, PACK):
+                    first_product(0, t)
+            if i == 1:
                 for t in range(PACK):
                     first_product(1, t)
             if pending is not None:
-                (b, j0, width, t0), values = pending
-                join(b, j0, width, t0, *values)
-                if t0 + STEP // width == PACK:
-                    quantize_z(b, j0, width)
+                (b, j0, width, count, t0), values = pending
+                last = j0 + width == PAIRS and b == 1
+                (join_last if last else join)(b, j0, width, count, t0, *values)
+                if t0 + count == PACK:
+                    quantize_z(b, j0, width, last)
                     if b == 1:
-                        second_product(j0, width, step is None)
+                        second_product(j0, width, last)
             pending = (step, picked)
 
         for q in range(4):

@@ -22,6 +22,7 @@ PASS = P * PACK
 BANK = 512
 CHUNK = 128
 LIST_ROWS = 16
+WIDE_STEP = 1024
 UNITS = ((0, 0, 512, 2), (1, 0, 256, 4), (1, 256, 128, 4), (1, 384, 128, 2))
 
 
@@ -76,7 +77,8 @@ def tile_list_graft_union_features_kernel(
         nc.sync.dma_start(rg[:], rgain.rearrange("(b p t) -> p b t", b=2, t=PACK))
 
         def round_w1(pool, b, a, u, on_vector):
-            grouped = pool.tile([P, 2, P, PACK], BF16, name="w1_grouped%d%d%d" % (b, a, u), align_bytes=64)
+            tag = "w1_grouped%d%d%d" % (b, a, u)
+            grouped = pool.tile([P, 2, P, PACK], BF16, name=tag, tag=tag, align_bytes=64)
             src = w1_raw[b, a][:].rearrange("p j (m t) -> p m j t", t=PACK)[:, :, :, 2 * u : 2 * u + 2]
             dst = grouped[:].rearrange("p t m j -> p m j t")
             if on_vector:
@@ -170,8 +172,14 @@ def tile_list_graft_union_features_kernel(
                 cols = slice(i * width, (i + 1) * width)
                 nc.vector.tensor_copy(scion[:, cols], h[b, t0 + i][:].indirect(pos1_sb[:, entries]))
                 nc.vector.tensor_copy(stock[:, cols], h[b, t0 + i][:].indirect(pos2_sb[:, entries]))
-            weak = ring.tile([P, count * width], F32, name="weak")
-            strong = ring.tile([P, count * width], F32, name="strong")
+            if b == 0:
+                weak = body.tile([P, count * width], F32, name="weak", tag="w1_grouped11%d" % (t0 // 2), align_bytes=64)
+            else:
+                weak = ring.tile([P, count * width], F32, name="weak")
+            if (b, j0) == (1, 0):
+                strong = keep.tile([P, count * width], F32, name="strong", tag="z_c0_0", align_bytes=64)
+            else:
+                strong = ring.tile([P, count * width], F32, name="strong")
             bounded = ring.tile([P, count * width], F32, name="bounded")
             nc.vector.tensor_tensor(weak[:], scion[:], stock[:], ALU.min)
             nc.vector.tensor_tensor(strong[:], scion[:], stock[:], ALU.max)
@@ -180,7 +188,8 @@ def tile_list_graft_union_features_kernel(
 
         def join(b, j0, width, count, t0, strong, bounded):
             total = ring.tile([P, count * width], F32, name="total")
-            nc.vector.tensor_tensor(total[:], strong[:], bounded[:], ALU.add)
+            engine = nc.gpsimd if count * width == WIDE_STEP else nc.vector
+            engine.tensor_tensor(total[:], strong[:], bounded[:], ALU.add)
             if t0 == 0:
                 z_planes[b, j0] = keep.tile([P, PACK, width], BF16, name="z_planes%d_%d" % (b, j0))
             for i in range(count):
@@ -204,11 +213,13 @@ def tile_list_graft_union_features_kernel(
                     ALU.mult,
                 )
             else:
-                nc.scalar.copy(
-                    grouped[:].rearrange("p (c i) t -> p c t i", i=4),
-                    z_planes[b, j0][:].rearrange("p t (c i) -> p c t i", i=4),
-                )
-            codes = keep.tile([P, width], U32, name="z_c%d_%d" % (b, j0), align_bytes=64)
+                for c0 in range(0, width, 256):
+                    cols = slice(c0, min(c0 + 256, width))
+                    nc.scalar.copy(
+                        grouped[:, cols, :].rearrange("p (c i) t -> p c t i", i=4),
+                        z_planes[b, j0][:, :, cols].rearrange("p t (c i) -> p c t i", i=4),
+                    )
+            codes = keep.tile([P, width], U32, name="z_c%d_%d" % (b, j0), tag="z_c%d_%d" % (b, j0), align_bytes=64)
             scales = keep.tile([P, width], U8, name="z_s%d_%d" % (b, j0), align_bytes=64)
             nc.vector.quantize_mx(codes[:].bitcast(FP8X4), scales[:], grouped[:].rearrange("p c t -> p (c t)"))
             for c0 in range(0, width, CHUNK):
@@ -236,7 +247,9 @@ def tile_list_graft_union_features_kernel(
                             start=(b == 0),
                             stop=(b == 1),
                         )
-                    if last:
+                    if last and t % 2:
+                        nc.vector.tensor_copy(y[:, t, :], sums[t])
+                    elif last:
                         nc.scalar.copy(y[:, t, :], sums[t])
                 if not last:
                     nc.scalar.copy(y[:, :, c0 : c0 + CHUNK], acc[:])
@@ -258,10 +271,9 @@ def tile_list_graft_union_features_kernel(
         for i, step in enumerate(steps + [None]):
             if i < 2:
                 later_w1 = [round_w1(body, 1, a, i, False) for a in range(2)]
-            picked = pick(*step) if step is not None else None
-            if i < 2:
                 for a in range(2):
                     quantize_w1(1, a, i, later_w1[a])
+            picked = pick(*step) if step is not None else None
             if i == 0:
                 for t in range(2, PACK):
                     first_product(0, t)
@@ -272,10 +284,11 @@ def tile_list_graft_union_features_kernel(
                 (b, j0, width, count, t0), values = pending
                 last = j0 + width == PAIRS and b == 1
                 (join_last if last else join)(b, j0, width, count, t0, *values)
-                if t0 + count == PACK:
+                if (b, j0) == (1, 0):
+                    quantize_z(0, 0, PAIRS, False)
+                if b == 1 and t0 + count == PACK:
                     quantize_z(b, j0, width, last)
-                    if b == 1:
-                        second_product(j0, width, last)
+                    second_product(j0, width, last)
             pending = (step, picked)
 
         for q in range(4):

from contextlib import ExitStack

import concourse.mybir as mybir

K, T, S, PAIRS, H, N = 1024, 4096, 1024, 512, 1024, 512
FLOPS = 2 * K * H * S + 2 * H * N * PAIRS

F32 = mybir.dt.float32
BF16 = mybir.dt.bfloat16
I32 = mybir.dt.int32
U32 = mybir.dt.uint32
U16 = mybir.dt.uint16
U8 = mybir.dt.uint8
FP8X4 = mybir.dt.float8_e4m3fn_x4
FP4X4 = mybir.dt.float4_e2m1fn_x4
ALU = mybir.AluOpType
ACT = mybir.ActivationFunctionType

P = 128
PACK = 4
PASS = P * PACK
BANK = 512
CHUNK = 128
LIST_ROWS = 16
WIDE_STEP = 1024
UNITS = ((0, 0, 512, 2), (1, 0, 256, 4), (1, 256, 128, 4), (1, 384, 128, 2))


def tile_list_graft_union_features_kernel(
    tc, tab_words, tab_scales, offs, pos1, pos2, w1, rgain, ugain, w2_words, w2_scales, out_0, out_1, out_2
):
    nc = tc.nc
    with ExitStack() as ctx:
        keep = ctx.enter_context(tc.tile_pool(name="keep", bufs=1))
        ring = ctx.enter_context(tc.tile_pool(name="ring", bufs=2))
        shared = ctx.enter_context(tc.tile_pool(name="shared", bufs=1))
        psum_h = ctx.enter_context(tc.psum_pool(name="psum_h", bufs=6))
        psum_y = ctx.enter_context(tc.psum_pool(name="psum_y", bufs=2))

        offs_sb = keep.tile([P, S // LIST_ROWS], U16, name="offs_sb")
        pos1_sb = keep.tile([P, PAIRS // LIST_ROWS], U16, name="pos1_sb")
        pos2_sb = keep.tile([P, PAIRS // LIST_ROWS], U16, name="pos2_sb")
        tab_w = [shared.tile([P, T], U16, name="tab_w0", align_bytes=64, offset=0)]
        tab_s = shared.tile([P, T], U8, name="tab_s", align_bytes=64, offset=2 * T)
        moved_s = keep.tile([P, S], U8, name="v_s1", align_bytes=64)
        w1_raw = {}
        w1_c = {}
        w1_s = {}
        y_s = keep.tile([P, PAIRS], U8, name="y_s", align_bytes=64)

        nc.vector.memset(tab_s[:, : T // 2].bitcast(I32), 0)
        nc.gpsimd.memset(tab_s[:, T // 2 :].bitcast(I32), 0)
        with tc.tile_pool(name="early", bufs=1) as early:
            warm = early.tile([P, 1], F32, name="warm")
            nc.gpsimd.memset(warm[:], 0.0)
            nc.scalar.activation(warm[:], warm[:], ACT.Tanh)
        late = ctx.enter_context(tc.tile_pool(name="late", bufs=1))
        tab_w.append(late.tile([P, T], U16, name="tab_w1", tag="second", align_bytes=64))
        rg = late.tile([P, 2, PACK], F32, name="rg")
        nc.gpsimd.memset(moved_s[:].bitcast(I32), 0)

        def load_w1(b, a, tag):
            w1_raw[b, a] = late.tile([P, PACK, PASS], F32, name="w1_raw%d%d" % (b, a), tag=tag, align_bytes=64)
            rows = w1[a * PASS : (a + 1) * PASS, b * PASS : (b + 1) * PASS]
            nc.sync.dma_start(w1_raw[b, a][:], rows.rearrange("(p j) c -> p j c", j=PACK))

        nc.sync.dma_start(offs_sb[:], offs)
        nc.sync.dma_start(pos1_sb[:], pos1)
        nc.sync.dma_start(pos2_sb[:], pos2)
        nc.sync.dma_start(tab_w[0][:].bitcast(I32), tab_words[0].bitcast(I32))
        for r in range(4):
            rows = tab_scales.bitcast(I32).rearrange("a (q r) n -> r q a n", r=4)[r]
            nc.sync.dma_start(tab_s[r:P:16, :].bitcast(I32), rows)
        load_w1(0, 0, "first")
        nc.sync.dma_start(tab_w[1][:].bitcast(I32), tab_words[1].bitcast(I32))
        load_w1(0, 1, "third")
        nc.sync.dma_start(rg[:], rgain.rearrange("(b p t) -> p b t", b=2, t=PACK))

        def round_w1(pool, b, a, u, on_vector):
            tag = "w1_grouped%d%d%d" % (b, a, u)
            grouped = pool.tile([P, 2, P, PACK], BF16, name=tag, tag=tag, align_bytes=64)
            src = w1_raw[b, a][:].rearrange("p j (m t) -> p m j t", t=PACK)[:, :, :, 2 * u : 2 * u + 2]
            dst = grouped[:].rearrange("p t m j -> p m j t")
            if on_vector:
                nc.vector.tensor_copy(dst, src)
            else:
                nc.scalar.copy(dst, src)
            return grouped

        def quantize_w1(b, a, u, grouped):
            w1_c[b, a, u] = keep.tile([P, 2 * P], U32, name="w1_c%d%d%d" % (b, a, u), align_bytes=64)
            if (b, a) == (0, 0):
                w1_s[b, a, u] = shared.tile([P, 2 * P], U8, name="w1_s00%d" % u, align_bytes=64, offset=2 * T + 256 * u)
            else:
                w1_s[b, a, u] = keep.tile([P, 2 * P], U8, name="w1_s%d%d%d" % (b, a, u), align_bytes=64)
            nc.vector.quantize_mx(
                w1_c[b, a, u][:].bitcast(FP8X4), w1_s[b, a, u][:], grouped[:].rearrange("p t m j -> p (t m j)")
            )

        h = {}

        def first_product(b, t):
            h[b, t] = keep.tile([P, S], F32, name="h%d%d" % (b, t))
            u, cols = t // 2, slice((t % 2) * P, (t % 2 + 1) * P)
            for m0 in range(0, S, BANK):
                acc = psum_h.tile([P, BANK], F32, name="acc_h")
                for a in range(2):
                    nc.tensor.matmul_mx(
                        acc[:],
                        lhsT=w1_c[b, a, u][:, cols].bitcast(FP8X4),
                        lhsT_scale=w1_s[b, a, u][:, cols],
                        rhs=v_w[a][:, m0 : m0 + BANK].bitcast(FP4X4),
                        rhs_scale=v_s[a][:, m0 : m0 + BANK],
                        start=(a == 0),
                        stop=(a == 1),
                    )
                nc.scalar.activation(h[b, t][:, m0 : m0 + BANK], acc[:], ACT.Copy, scale=rg[:, b, t : t + 1])

        def deal_w2(a):
            nc.vector.tensor_copy(
                w2w[a][:].bitcast(U16).rearrange("p (r q) -> p r q", r=PACK),
                w2w_raw[:, a, :].bitcast(U16).rearrange("p (q r) -> p r q", r=PACK),
            )
            nc.vector.tensor_copy(
                w2s[a][:].rearrange("p (r q) -> p r q", r=PACK),
                w2s_raw[:, a, :].rearrange("p (q r) -> p r q", r=PACK),
            )

        w2s_raw = late.tile([P, 2, N], U8, name="w2s_raw", align_bytes=64)
        w2w_raw = late.tile([P, 2, 2 * N], U8, name="w2w_raw", align_bytes=64)
        nc.gpsimd.memset(w2s_raw[:].rearrange("p a n -> p (a n)").bitcast(I32), 0)
        nc.sync.dma_start(w2w_raw[:].bitcast(I32), w2_words.bitcast(I32).rearrange("a p n -> p a n"))
        for q in range(4):
            nc.sync.dma_start(
                w2s_raw[32 * q : 32 * q + 4, :, :].bitcast(I32),
                w2_scales.bitcast(I32)[:, 4 * q : 4 * q + 4, :].rearrange("a r n -> r a n"),
            )
        v_w = [keep.tile([P, S], U16, name="v_w0", align_bytes=64)]
        nc.vector.tensor_copy(v_w[0][:], tab_w[0][:].indirect(offs_sb[:]))
        v_s = [shared.tile([P, S], U8, name="v_s0", align_bytes=64, offset=0), moved_s]
        nc.vector.tensor_copy(v_s[0][:], tab_s[:].indirect(offs_sb[:]))
        nc.sync.dma_start(v_s[1][0:100, :].bitcast(I32), v_s[0][16:116, :].bitcast(I32))
        with tc.tile_pool(name="head", bufs=1) as head:
            first = [round_w1(head, 0, 0, u, False) for u in range(2)]
            v_w.append(shared.tile([P, S], U16, name="v_w1", align_bytes=64, offset=2 * T + 512))
            nc.vector.tensor_copy(v_w[1][:], tab_w[1][:].indirect(offs_sb[:]))
            for u in range(2):
                quantize_w1(0, 0, u, first[u])
            load_w1(1, 0, "first")
            load_w1(1, 1, "second")
            quantize_w1(0, 1, 0, round_w1(head, 0, 1, 0, False))
        quantize_w1(0, 1, 1, round_w1(late, 0, 1, 1, False))
        body = ctx.enter_context(tc.tile_pool(name="body", bufs=1))
        ug = body.tile([P, 2, PACK], F32, name="ug")
        nc.sync.dma_start(ug[:], ugain.rearrange("(b p t) -> p b t", b=2, t=PACK))
        w2w = [body.tile([P, 2 * N], U8, name="w2w%d" % a, align_bytes=64) for a in range(2)]
        w2s = [body.tile([P, N], U8, name="w2s%d" % a, align_bytes=64) for a in range(2)]
        for t in range(2):
            first_product(0, t)
        for a in range(2):
            deal_w2(a)

        z_planes = {}
        z_c = {}
        z_s = {}

        def pick(b, j0, width, count, t0):
            scion = ring.tile([P, count * width], F32, name="scion")
            stock = ring.tile([P, count * width], F32, name="stock")
            entries = slice(j0 // LIST_ROWS, (j0 + width) // LIST_ROWS)
            for i in range(count):
                cols = slice(i * width, (i + 1) * width)
                nc.vector.tensor_copy(scion[:, cols], h[b, t0 + i][:].indirect(pos1_sb[:, entries]))
                nc.vector.tensor_copy(stock[:, cols], h[b, t0 + i][:].indirect(pos2_sb[:, entries]))
            if b == 0:
                weak = body.tile([P, count * width], F32, name="weak", tag="w1_grouped11%d" % (t0 // 2), align_bytes=64)
            else:
                weak = ring.tile([P, count * width], F32, name="weak")
            if (b, j0) == (1, 0):
                strong = keep.tile([P, count * width], F32, name="strong", tag="z_c0_0", align_bytes=64)
            else:
                strong = ring.tile([P, count * width], F32, name="strong")
            bounded = ring.tile([P, count * width], F32, name="bounded")
            nc.vector.tensor_tensor(weak[:], scion[:], stock[:], ALU.min)
            nc.vector.tensor_tensor(strong[:], scion[:], stock[:], ALU.max)
            nc.scalar.activation(bounded[:], weak[:], ACT.Tanh)
            return strong, bounded

        def join(b, j0, width, count, t0, strong, bounded):
            total = ring.tile([P, count * width], F32, name="total")
            engine = nc.gpsimd if count * width == WIDE_STEP else nc.vector
            engine.tensor_tensor(total[:], strong[:], bounded[:], ALU.add)
            if t0 == 0:
                z_planes[b, j0] = keep.tile([P, PACK, width], BF16, name="z_planes%d_%d" % (b, j0))
            for i in range(count):
                t = t0 + i
                nc.scalar.activation(
                    z_planes[b, j0][:, t, :], total[:, i * width : (i + 1) * width], ACT.Copy, scale=ug[:, b, t : t + 1]
                )

        def join_last(b, j0, width, count, t0, strong, bounded):
            if t0 == 0:
                z_planes[b, j0] = keep.tile([P, PACK * width], F32, name="z_sums")
            nc.vector.tensor_tensor(z_planes[b, j0][:, t0 * width : (t0 + count) * width], strong[:], bounded[:], ALU.add)

        def quantize_z(b, j0, width, last):
            grouped = keep.tile([P, width, PACK], BF16, name="z_grouped%d_%d" % (b, j0), align_bytes=64)
            if last:
                nc.vector.tensor_tensor(
                    grouped[:].rearrange("p (c i) t -> p c t i", i=2),
                    z_planes[b, j0][:].rearrange("p (t c i) -> p c t i", t=PACK, i=2),
                    ug[:, b, :].unsqueeze(1).unsqueeze(3).to_broadcast([P, width // 2, PACK, 2]),
                    ALU.mult,
                )
            else:
                for c0 in range(0, width, 256):
                    cols = slice(c0, min(c0 + 256, width))
                    nc.scalar.copy(
                        grouped[:, cols, :].rearrange("p (c i) t -> p c t i", i=4),
                        z_planes[b, j0][:, :, cols].rearrange("p t (c i) -> p c t i", i=4),
                    )
            codes = keep.tile([P, width], U32, name="z_c%d_%d" % (b, j0), tag="z_c%d_%d" % (b, j0), align_bytes=64)
            scales = keep.tile([P, width], U8, name="z_s%d_%d" % (b, j0), align_bytes=64)
            nc.vector.quantize_mx(codes[:].bitcast(FP8X4), scales[:], grouped[:].rearrange("p c t -> p (c t)"))
            for c0 in range(0, width, CHUNK):
                z_c[b, j0 + c0] = codes[:, c0 : c0 + CHUNK]
                z_s[b, j0 + c0] = scales[:, c0 : c0 + CHUNK]

        def second_product(j0, width, last):
            y = keep.tile([P, PACK, width], F32, name="y%d" % j0)
            grouped = keep.tile([P, width, PACK], BF16, name="y_grouped%d" % j0, align_bytes=64)
            codes = keep.tile([P, width], U32, name="y_c%d" % j0, align_bytes=64)
            for c0 in range(0, width, CHUNK):
                if last:
                    sums = [psum_h.tile([P, BANK], F32, name="acc_h")[:, :CHUNK] for t in range(PACK)]
                else:
                    acc = psum_y.tile([P, PACK, CHUNK], F32, name="acc_y")
                    sums = [acc[:, t, :] for t in range(PACK)]
                for t in range(PACK):
                    for b in range(2):
                        nc.tensor.matmul_mx(
                            sums[t],
                            lhsT=w2w[b][:, 2 * P * t : 2 * P * (t + 1)].bitcast(FP4X4),
                            lhsT_scale=w2s[b][:, P * t : P * (t + 1)],
                            rhs=z_c[b, j0 + c0].bitcast(FP8X4),
                            rhs_scale=z_s[b, j0 + c0],
                            start=(b == 0),
                            stop=(b == 1),
                        )
                    if last and t % 2:
                        nc.vector.tensor_copy(y[:, t, :], sums[t])
                    elif last:
                        nc.scalar.copy(y[:, t, :], sums[t])
                if not last:
                    nc.scalar.copy(y[:, :, c0 : c0 + CHUNK], acc[:])
            dst = grouped[:].rearrange("p (c i) t -> p c t i", i=4)
            src = y[:].rearrange("p t (c i) -> p c t i", i=4)
            if last:
                nc.vector.tensor_copy(dst, src)
            else:
                nc.scalar.copy(dst, src)
            nc.sync.dma_start(out_0.rearrange("(p t) j -> p t j", t=PACK)[:, :, j0 : j0 + width], y[:])
            nc.vector.quantize_mx(
                codes[:].bitcast(FP8X4), y_s[:, j0 : j0 + width], grouped[:].rearrange("p c t -> p (c t)")
            )
            words = out_1[0].rearrange("p m t -> p (m t)")[:, PACK * j0 : PACK * (j0 + width)]
            (nc.scalar if last else nc.sync).dma_start(words.bitcast(I32), codes[:].bitcast(I32))

        steps = [unit + (t0,) for unit in UNITS for t0 in range(0, PACK, unit[3])]
        pending = None
        for i, step in enumerate(steps + [None]):
            if i < 2:
                later_w1 = [round_w1(body, 1, a, i, False) for a in range(2)]
                for a in range(2):
                    quantize_w1(1, a, i, later_w1[a])
            picked = pick(*step) if step is not None else None
            if i == 0:
                for t in range(2, PACK):
                    first_product(0, t)
            if i == 1:
                for t in range(PACK):
                    first_product(1, t)
            if pending is not None:
                (b, j0, width, count, t0), values = pending
                last = j0 + width == PAIRS and b == 1
                (join_last if last else join)(b, j0, width, count, t0, *values)
                if (b, j0) == (1, 0):
                    quantize_z(0, 0, PAIRS, False)
                if b == 1 and t0 + count == PACK:
                    quantize_z(b, j0, width, last)
                    second_product(j0, width, last)
            pending = (step, picked)

        for q in range(4):
            engine = nc.scalar if q % 2 else nc.sync
            engine.dma_start(out_2[0, 4 * q : 4 * q + 4, :].bitcast(I32), y_s[32 * q : 32 * q + 4, :].bitcast(I32))
